import numpy as np
import ml_dtypes


def mxq(x, axis, fmt="e4m3"):
    dtype, down = {"e4m3": (ml_dtypes.float8_e4m3fn, 7), "e5m2": (ml_dtypes.float8_e5m2, 14)}[fmt]
    v = np.moveaxis(np.asarray(x, np.float32).astype(ml_dtypes.bfloat16).astype(np.float64), axis, -1)
    blocks = v.reshape(v.shape[:-1] + (-1, 32))
    amax = np.abs(blocks).max(-1, keepdims=True)
    byte = np.maximum(np.where(amax > 0, np.frexp(amax)[1] - 1 + 127, 0) - down, 1)
    scale = np.exp2(byte - 127.0)
    codes = (blocks / scale).astype(np.float32).astype(dtype).astype(np.float64)
    return np.moveaxis((codes * scale).reshape(v.shape), -1, axis)


WIDE = False


def mx_kscale(k):
    if not WIDE:
        return np.ones(k)
    levels = np.array([10, -10, 5, -5, 0])
    if k % 512:
        return np.exp2(np.random.permutation(np.resize(levels, k // 32))).repeat(32)
    a = np.empty((k // 512, 16))
    for p in range(k // 512):
        a[p, :8] = np.random.permutation(np.resize(levels, 8))
        for g in range(8):
            far = levels[np.abs(levels - a[p, g]) >= 10]
            a[p, g + 8] = far[np.random.randint(len(far))]
    return np.exp2(a.ravel()).repeat(32)


def f64(x):
    return np.asarray(x).astype(np.float64)


def striped(idx):
    return np.tile(idx.reshape(-1, 16).T, (8, 1)).astype(np.uint16)


def unstriped(offs):
    return offs[:16].T.reshape(-1).astype(np.int64)


E2M1 = np.array([0.0, 0.5, 1.0, 1.5, 2.0, 3.0, 4.0, 6.0, -0.0, -0.5, -1.0, -1.5, -2.0, -3.0, -4.0, -6.0])


def pack_weight(w, fmt):
    k, n = w.shape
    w = f64(np.asarray(w, np.float32).astype(ml_dtypes.bfloat16)).reshape(k // 32, 32, n)
    amax = np.abs(w).max(1)
    if fmt == "e4m3":
        byte = np.frexp(amax)[1] - 1 + 127 - 7
    else:
        mant, ex = np.frexp(amax / 6.0)
        byte = np.where(mant > 0.5, ex, ex - 1) + 127
    byte = np.clip(np.where(amax > 0, byte, 1), 1, 254)
    scaled = (w * np.exp2(127.0 - byte)[:, None, :]).reshape(k, n).astype(np.float32)
    by_word = np.ascontiguousarray(scaled.reshape(k // 512, 128, 4, n).transpose(0, 1, 3, 2))
    if fmt == "e4m3":
        words = by_word.astype(ml_dtypes.float8_e4m3fn).view(np.uint8)
    else:
        c = by_word.astype(ml_dtypes.float4_e2m1fn).view(np.uint8) & 0xF
        words = (c[..., 0::2] | (c[..., 1::2] << 4)).reshape(k // 512, 128, 2 * n)
    return np.ascontiguousarray(words), np.ascontiguousarray(byte.astype(np.uint8).reshape(k // 512, 16, n))


def unpack_weight(words, scales, fmt):
    g, _, n = scales.shape
    words = np.ascontiguousarray(words).reshape(g, 128, n, -1)
    if fmt == "e4m3":
        vals = words.view(ml_dtypes.float8_e4m3fn).astype(np.float64)
    else:
        nib = np.empty((g, 128, n, 4), np.uint8)
        nib[..., 0::2] = words & 0xF
        nib[..., 1::2] = words >> 4
        vals = E2M1[nib]
    vals = vals * np.repeat(np.exp2(scales.astype(np.float64) - 127.0), 8, axis=1)[..., None]
    return vals.transpose(0, 1, 3, 2).reshape(g * 512, n)


def gelu(v):
    return 0.5 * v * (1.0 + np.tanh(np.sqrt(2.0 / np.pi) * (v + 0.044715 * v**3)))


def striped8(idx):
    return np.concatenate([v.reshape(-1, 16).T for v in idx]).astype(np.uint16)


def unstriped8(offs):
    return np.stack([offs[16 * g:16 * g + 16].T.reshape(-1) for g in range(8)]).astype(np.int64)


def heads(h, wgt, idx8):
    r = np.arange(h.shape[0])
    return wgt[r // 4 % 128] * h[r[:, None], idx8[r % 512 // 64]]


K, T, S, H, P, N = 1024, 4096, 1024, 1536, 512, 384


def setup_inputs():
    n = np.random.standard_normal
    s = mx_kscale(K)[:, None]
    u = mx_kscale(H)[:, None]
    tab_words, tab_scales = pack_weight(n((K, T)) * s, "e4m3")
    w1 = 1.4 * n((K, H)) / np.sqrt(K) / s
    w4_words, w4_scales = pack_weight(n((H, N)) / np.sqrt(H) / u**2, "e2m1")
    return {
        "tab_words": tab_words, "tab_scales": tab_scales,
        "offs": striped(np.random.permutation(T)[:S]),
        "w1": w1.astype(np.float32),
        "gain": (np.exp(0.3 * n(H)) * u[:, 0]).astype(np.float32),
        "offs2": striped8(np.stack([np.random.permutation(S)[:P] for _ in range(8)])),
        "offs3": striped8(np.stack([np.random.permutation(S)[:P] for _ in range(8)])),
        "wga": np.repeat(np.random.uniform(0.5, 2.0, (8, P)), 16, axis=0).astype(np.float32),
        "wgb": np.repeat(np.random.uniform(0.5, 2.0, (8, P)), 16, axis=0).astype(np.float32),
        "w4_words": w4_words, "w4_scales": w4_scales,
    }


def reference(tab_words, tab_scales, offs, w1, gain, offs2, offs3, wga, wgb, w4_words, w4_scales):
    v = unpack_weight(tab_words, tab_scales, "e4m3")[:, unstriped(offs)]
    h = f64(gain)[:, None] * np.tanh(mxq(f64(w1), 0, "e4m3").T @ v)
    xa = heads(h, f64(wga), unstriped8(offs2))
    xb = heads(h, f64(wgb), unstriped8(offs3))
    z = (xa - xb) * np.maximum(xa, xb)
    w4 = unpack_weight(w4_words, w4_scales, "e2m1")
    y = w4.T @ mxq(z, 0, "e4m3")
    return np.sqrt(np.abs(y))

@@ -1,0 +1,294 @@
+from contextlib import ExitStack
+
+import concourse.mybir as mybir
+from concourse.masks import make_identity
+
+K, T, S, H, M, N = 1024, 4096, 1024, 1536, 512, 384
+FLOPS = 2 * K * H * S + 2 * H * N * M
+
+F32 = mybir.dt.float32
+BF16 = mybir.dt.bfloat16
+I32 = mybir.dt.int32
+U32 = mybir.dt.uint32
+U16 = mybir.dt.uint16
+U8 = mybir.dt.uint8
+FP8X4 = mybir.dt.float8_e4m3fn_x4
+FP4X4 = mybir.dt.float4_e2m1fn_x4
+ALU = mybir.AluOpType
+ACT = mybir.ActivationFunctionType
+
+P = 128
+PACK = 4
+K_PASS = P * PACK
+BANK = 512
+KP = K // K_PASS
+HP = H // K_PASS
+CHUNKS = M // P
+GAIN_ON_VECTOR = 2
+
+
+def tile_list_reassortment_watch_scores_kernel(
+    tc, tab_words, tab_scales, offs, w1, gain, offs2, offs3, wga, wgb, w4_words, w4_scales, out
+):
+    nc = tc.nc
+    with ExitStack() as ctx:
+        held = ctx.enter_context(tc.tile_pool(name="held", bufs=1))
+        two = ctx.enter_context(tc.tile_pool(name="two", bufs=2))
+        four = ctx.enter_context(tc.tile_pool(name="four", bufs=4))
+        slots = ctx.enter_context(tc.tile_pool(name="slots", bufs=1))
+        psum = ctx.enter_context(tc.psum_pool(name="psum", bufs=1))
+
+        list1 = held.tile([P, S // 16], U16, name="list1")
+        list2 = held.tile([P, M // 16], U16, name="list2")
+        list3 = held.tile([P, M // 16], U16, name="list3")
+        nc.sync.dma_start(list1[:], offs)
+
+        ident = held.tile([P, P], F32, name="ident")
+        make_identity(nc, ident[:])
+
+        tab_s = slots.tile([P, T], U8, name="tab_s", tag="tab_s", align_bytes=64)
+        nc.vector.memset(tab_s[:].bitcast(I32), 0)
+        for q in range(4):
+            nc.gpsimd.dma_start(
+                tab_s[32 * q : 32 * q + 4 * KP, :].bitcast(I32),
+                tab_scales[:, 4 * q : 4 * q + 4, :].bitcast(I32),
+            )
+        tab_w = []
+        for a in range(KP):
+            words = held.tile([P, T], U32, name="tab_w%d" % a, align_bytes=64)
+            nc.sync.dma_start(words[:].bitcast(I32), tab_words[a].rearrange("p t i -> p (t i)").bitcast(I32))
+            tab_w.append(words)
+
+        def load_w1(b):
+            if b == 0:
+                parts = [held.tile([P, PACK, K_PASS], F32, name="raw0%d" % a)[:] for a in range(KP)]
+                whole = None
+            else:
+                whole = held.tile([P, KP, PACK, K_PASS], F32, name="raw%d" % b)
+                parts = [whole[:, a] for a in range(KP)]
+            for a in range(KP):
+                rows = w1[a * K_PASS : (a + 1) * K_PASS, b * K_PASS : (b + 1) * K_PASS]
+                nc.sync.dma_start(parts[a], rows.rearrange("(p j) c -> p j c", j=PACK))
+            return parts if b == 0 else whole
+
+        raw_w1 = {0: load_w1(0)}
+
+        gain_sb = held.tile([P, HP, PACK], F32, name="gain_sb")
+        nc.gpsimd.dma_start(gain_sb[:], gain.rearrange("(b p i) -> p b i", p=P, i=PACK))
+        wa = held.tile([P, M], F32, name="wa")
+        wb = held.tile([P, M], F32, name="wb")
+        nc.sync.dma_start(list2[:], offs2)
+        nc.sync.dma_start(wa[:], wga)
+        nc.sync.dma_start(list3[:], offs3)
+        nc.sync.dma_start(wb[:], wgb)
+        raw_w1[1] = load_w1(1)
+
+        w4_s = held.tile([P, HP, N], U8, name="w4_s", align_bytes=64)
+        nc.vector.memset(w4_s[:].rearrange("p b n -> p (b n)").bitcast(I32), 0)
+        for q in range(4):
+            nc.gpsimd.dma_start(
+                w4_s[32 * q : 32 * q + 4, :, :].bitcast(I32),
+                w4_scales[:, 4 * q : 4 * q + 4, :].rearrange("b r n -> r b n").bitcast(I32),
+            )
+        w4_w = held.tile([P, HP, 2 * N], U8, name="w4_w", align_bytes=64)
+        nc.sync.dma_start(w4_w[:].bitcast(I32), w4_words.rearrange("b p c -> p b c").bitcast(I32))
+        raw_w1[2] = load_w1(2)
+
+        v_w = [held.tile([P, S], U32, name="v_w0", align_bytes=64)]
+        v_s = held.tile([P, S], U8, name="v_s", align_bytes=64)
+        nc.vector.tensor_copy(v_w[0][:], tab_w[0][:].indirect(list1[:]))
+        nc.vector.tensor_copy(v_s[:], tab_s[:].indirect(list1[:]))
+        v_w.append(slots.tile([P, S], U32, name="v_w1", tag="tab_s", align_bytes=64))
+        nc.vector.tensor_copy(v_w[1][:], tab_w[1][:].indirect(list1[:]))
+
+        w1_q = {}
+        banks_used = []
+
+        def next_bank(shape, name):
+            bank = psum.tile(shape, F32, name=name, tag="work%d" % (len(banks_used) % 4))
+            banks_used.append(name)
+            return bank
+
+        def prepare_first_w1(a, u):
+            pairs = raw_w1[0][a].rearrange("p j (m u t) -> p u m j t", u=2, t=2)
+            woven = two.tile([P, 2 * K_PASS], BF16, name="woven0", align_bytes=64)
+            nc.vector.tensor_copy(woven[:].rearrange("p (t m j) -> p m j t", t=2, j=PACK), pairs[:, u])
+            codes = held.tile([P, 2 * P], U32, name="w1_c0%d%d" % (a, u), align_bytes=64)
+            scales = held.tile([P, 2 * P], U8, name="w1_s0%d%d" % (a, u), align_bytes=64)
+            nc.vector.quantize_mx(out=codes[:].bitcast(FP8X4), scales=scales[:], in_=woven[:])
+            w1_q[0, a, u] = (codes[:], scales[:])
+
+        def prepare_w1(b, u):
+            pairs = raw_w1[b][:].rearrange("p a j (m u t) -> p u a m j t", u=2, t=2)
+            woven = slots.tile([P, KP * 2 * K_PASS], BF16, name="woven", tag="h%d%d" % (b - 1, u + 1), align_bytes=64)
+            nc.scalar.copy(woven[:].rearrange("p (a t m j) -> p a m j t", a=KP, t=2, j=PACK), pairs[:, u])
+            codes = held.tile([P, KP * 2 * P], U32, name="w1_c%d%d" % (b, u), align_bytes=64)
+            scales = held.tile([P, KP * 2 * P], U8, name="w1_s%d%d" % (b, u), align_bytes=64)
+            nc.vector.quantize_mx(out=codes[:].bitcast(FP8X4), scales=scales[:], in_=woven[:])
+            for a in range(KP):
+                w1_q[b, a, u] = (codes[:, a * 2 * P : (a + 1) * 2 * P], scales[:, a * 2 * P : (a + 1) * 2 * P])
+
+        h_tiles = {}
+
+        def make_h(b, i):
+            h = slots.tile([P, S], F32, name="h", tag="h%d%d" % (b % 2, i), align_bytes=64)
+            cols = slice((i % 2) * P, (i % 2 + 1) * P)
+            factor = gain_sb[:, b, i : i + 1]
+            on_vector = PACK * b + i < GAIN_ON_VECTOR
+            for s0 in range(0, S, BANK):
+                acc = next_bank([P, BANK], "acc")
+                for a in range(KP):
+                    codes, scales = w1_q[b, a, i // 2]
+                    nc.tensor.matmul_mx(
+                        out=acc[:],
+                        lhsT=codes[:, cols].bitcast(FP8X4),
+                        lhsT_scale=scales[:, cols],
+                        rhs=v_w[a][:, s0 : s0 + BANK].bitcast(FP8X4),
+                        rhs_scale=v_s[4 * a :, s0 : s0 + BANK],
+                        start=(a == 0),
+                        stop=(a == KP - 1),
+                    )
+                nc.scalar.activation(h[:, s0 : s0 + BANK], acc[:], ACT.Tanh)
+                if on_vector:
+                    nc.vector.tensor_scalar(h[:, s0 : s0 + BANK], h[:, s0 : s0 + BANK], factor, None, ALU.mult)
+            if not on_vector:
+                nc.scalar.activation(h[:], h[:], ACT.Copy, scale=factor)
+            h_tiles[b, i] = h
+
+        neg_wb = held.tile([P, M], F32, name="neg_wb")
+        xa_first = {}
+        xa = {}
+        neg_xb = {}
+
+        def pick(b, i):
+            if i == 0:
+                xa_first[b] = two.tile([P, PACK - 1, M], F32, name="xa_first")
+                neg_xb[b] = two.tile([P, PACK, M], F32, name="neg_xb")
+            if i < PACK - 1:
+                xa[b, i] = xa_first[b][:, i, :]
+            else:
+                last = slots.tile([P, M], F32, name="xa_last", tag="h%d1" % (b % 2), align_bytes=64)
+                xa[b, i] = last[:]
+            h = h_tiles[b, i]
+            nc.vector.tensor_tensor(xa[b, i], h[:].indirect(list2[:]), wa[:], ALU.mult)
+            nc.vector.tensor_tensor(neg_xb[b][:, i, :], h[:].indirect(list3[:]), neg_wb[:], ALU.mult)
+
+        larger = {}
+
+        def take_larger(b):
+            big = slots.tile([P, PACK, M], F32, name="big", tag="h%d%d" % (b % 2, PACK - 1), align_bytes=64)
+            flat = "p i m -> p (i m)"
+            nc.vector.scalar_tensor_tensor(
+                big[:, : PACK - 1, :].rearrange(flat),
+                neg_xb[b][:, : PACK - 1, :].rearrange(flat),
+                -1.0,
+                xa_first[b][:].rearrange(flat),
+                ALU.mult,
+                ALU.max,
+            )
+            nc.vector.scalar_tensor_tensor(
+                big[:, PACK - 1, :], neg_xb[b][:, PACK - 1, :], -1.0, xa[b, PACK - 1], ALU.mult, ALU.max
+            )
+            larger[b] = big
+
+        diffs = {}
+
+        def take_difference(b, i):
+            turned = next_bank([P, CHUNKS, P], "turned")
+            for c in range(CHUNKS):
+                cols = slice(c * P, (c + 1) * P)
+                nc.tensor.matmul(turned[:, c, :], xa[b, i][:, cols], ident[:], is_transpose=True, start=True, stop=False)
+                nc.tensor.matmul(turned[:, c, :], neg_xb[b][:, i, cols], ident[:], is_transpose=True, start=False, stop=True)
+            staged = four.tile([P, CHUNKS, P], F32, name="staged")
+            nc.scalar.copy(staged[:], turned[:])
+            for c in range(CHUNKS):
+                if i == 0:
+                    diffs[b, c] = psum.tile([P, PACK, P], F32, name="diff", tag="diff%d" % c)
+                nc.tensor.transpose(diffs[b, c][:, i, :], staged[:, c, :], ident[:])
+
+        def multiply(b, c, z_cols):
+            walk = "p i (c j) -> p c i j"
+            nc.vector.tensor_tensor(
+                z_cols.rearrange("p (c j i) -> p c i j", j=2, i=PACK),
+                diffs[b, c][:].rearrange(walk, j=2),
+                larger[b][:, :, c * P : (c + 1) * P].rearrange(walk, j=2),
+                ALU.mult,
+            )
+
+        z_q = {}
+
+        def quantize_z(b, c0, z):
+            width = z.shape[1] // PACK
+            codes = held.tile([P, width], U32, name="z_c%d%d" % (b, c0), align_bytes=64)
+            scales = held.tile([P, width], U8, name="z_s%d%d" % (b, c0), align_bytes=64)
+            nc.vector.quantize_mx(out=codes[:].bitcast(FP8X4), scales=scales[:], in_=z[:])
+            for c in range(width // P):
+                z_q[b, c0 + c] = (codes[:, c * P : (c + 1) * P], scales[:, c * P : (c + 1) * P])
+
+        def combine(b):
+            z = held.tile([P, PACK * M], BF16, name="z", align_bytes=64)
+            for c in range(CHUNKS):
+                multiply(b, c, z[:, c * PACK * P : (c + 1) * PACK * P])
+            quantize_z(b, 0, z)
+
+        y_banks = {}
+
+        def score_pass(b, c):
+            codes, scales = z_q[b, c]
+            if b == 0:
+                y_banks[c] = next_bank([P, N // P, P], "y")
+            for n in range(N // P):
+                nc.tensor.matmul_mx(
+                    out=y_banks[c][:, n, :],
+                    lhsT=w4_w[:, b, 2 * P * n : 2 * P * (n + 1)].bitcast(FP4X4),
+                    lhsT_scale=w4_s[:, b, P * n : P * (n + 1)],
+                    rhs=codes.bitcast(FP8X4),
+                    rhs_scale=scales,
+                    start=(b == 0 and n == 0),
+                    stop=(b == HP - 1 and n == N // P - 1),
+                )
+
+        def finish(c):
+            size = two.tile([P, N // P, P], F32, name="size")
+            nc.scalar.activation(size[:], y_banks[c][:], ACT.Abs)
+            root = four.tile([P, N // P, P], F32, name="root")
+            nc.scalar.activation(root[:], size[:], ACT.Sqrt)
+            nc.sync.dma_start(out[:, c * P : (c + 1) * P].rearrange("(n p) m -> p n m", p=P), root[:])
+
+        for a in range(KP):
+            for u in range(2):
+                prepare_first_w1(a, u)
+        nc.vector.tensor_scalar(neg_wb[:], wb[:], -1.0, None, ALU.mult)
+
+        last = HP - 1
+        for b in range(HP):
+            for i in range(PACK):
+                make_h(b, i)
+                if i < PACK - 1:
+                    pick(b, i)
+            if b < last:
+                prepare_w1(b + 1, 0)
+            pick(b, PACK - 1)
+            take_larger(b)
+            for i in range(PACK):
+                if b < last and i == 2:
+                    prepare_w1(b + 1, 1)
+                take_difference(b, i)
+            if b < last:
+                combine(b)
+
+        for c in range(CHUNKS):
+            for b in range(last):
+                score_pass(b, c)
+        z_last = []
+        for c in range(CHUNKS):
+            z = four.tile([P, PACK * P], BF16, name="z_last", align_bytes=64)
+            multiply(last, c, z[:])
+            z_last.append(z)
+            if c > 0:
+                quantize_z(last, c - 1, z_last[c - 1])
+                score_pass(last, c - 1)
+                finish(c - 1)
+        quantize_z(last, CHUNKS - 1, z_last[CHUNKS - 1])
+        score_pass(last, CHUNKS - 1)
+        finish(CHUNKS - 1)

@@ -35,6 +35,7 @@ def tile_list_reassortment_watch_scores_kernel(
         held = ctx.enter_context(tc.tile_pool(name="held", bufs=1))
         two = ctx.enter_context(tc.tile_pool(name="two", bufs=2))
         four = ctx.enter_context(tc.tile_pool(name="four", bufs=4))
+        shared = ctx.enter_context(tc.tile_pool(name="shared", bufs=1))
         slots = ctx.enter_context(tc.tile_pool(name="slots", bufs=1))
         psum = ctx.enter_context(tc.psum_pool(name="psum", bufs=1))
 
@@ -55,7 +56,7 @@ def tile_list_reassortment_watch_scores_kernel(
             )
         tab_w = []
         for a in range(KP):
-            words = held.tile([P, T], U32, name="tab_w%d" % a, align_bytes=64)
+            words = shared.tile([P, T], U32, name="tab_w%d" % a, align_bytes=64, offset=4 * T * a)
             nc.sync.dma_start(words[:].bitcast(I32), tab_words[a].rearrange("p t i -> p (t i)").bitcast(I32))
             tab_w.append(words)
 
@@ -74,10 +75,10 @@ def tile_list_reassortment_watch_scores_kernel(
         raw_w1 = {0: load_w1(0)}
 
         gain_sb = held.tile([P, HP, PACK], F32, name="gain_sb")
-        nc.gpsimd.dma_start(gain_sb[:], gain.rearrange("(b p i) -> p b i", p=P, i=PACK))
         wa = held.tile([P, M], F32, name="wa")
         wb = held.tile([P, M], F32, name="wb")
         nc.sync.dma_start(list2[:], offs2)
+        nc.sync.dma_start(gain_sb[:], gain.rearrange("(b p i) -> p b i", p=P, i=PACK))
         nc.sync.dma_start(wa[:], wga)
         nc.sync.dma_start(list3[:], offs3)
         nc.sync.dma_start(wb[:], wgb)
@@ -111,7 +112,9 @@ def tile_list_reassortment_watch_scores_kernel(
 
         def prepare_first_w1(a, u):
             pairs = raw_w1[0][a].rearrange("p j (m u t) -> p u m j t", u=2, t=2)
-            woven = two.tile([P, 2 * K_PASS], BF16, name="woven0", align_bytes=64)
+            woven = shared.tile(
+                [P, 2 * K_PASS], BF16, name="woven0%d%d" % (a, u), align_bytes=64, offset=4 * T + 4 * K_PASS * (2 * a + u)
+            )
             nc.vector.tensor_copy(woven[:].rearrange("p (t m j) -> p m j t", t=2, j=PACK), pairs[:, u])
             codes = held.tile([P, 2 * P], U32, name="w1_c0%d%d" % (a, u), align_bytes=64)
             scales = held.tile([P, 2 * P], U8, name="w1_s0%d%d" % (a, u), align_bytes=64)

@@ -35,7 +35,6 @@ def tile_list_reassortment_watch_scores_kernel(
         held = ctx.enter_context(tc.tile_pool(name="held", bufs=1))
         two = ctx.enter_context(tc.tile_pool(name="two", bufs=2))
         four = ctx.enter_context(tc.tile_pool(name="four", bufs=4))
-        shared = ctx.enter_context(tc.tile_pool(name="shared", bufs=1))
         slots = ctx.enter_context(tc.tile_pool(name="slots", bufs=1))
         psum = ctx.enter_context(tc.psum_pool(name="psum", bufs=1))
 
@@ -49,16 +48,17 @@ def tile_list_reassortment_watch_scores_kernel(
 
         tab_s = slots.tile([P, T], U8, name="tab_s", tag="tab_s", align_bytes=64)
         nc.vector.memset(tab_s[:].bitcast(I32), 0)
-        for q in range(4):
-            nc.gpsimd.dma_start(
-                tab_s[32 * q : 32 * q + 4 * KP, :].bitcast(I32),
-                tab_scales[:, 4 * q : 4 * q + 4, :].bitcast(I32),
-            )
         tab_w = []
         for a in range(KP):
-            words = shared.tile([P, T], U32, name="tab_w%d" % a, align_bytes=64, offset=4 * T * a)
+            words = held.tile([P, T], U32, name="tab_w%d" % a, align_bytes=64)
             nc.sync.dma_start(words[:].bitcast(I32), tab_words[a].rearrange("p t i -> p (t i)").bitcast(I32))
             tab_w.append(words)
+            if a == 0:
+                for q in range(4):
+                    nc.sync.dma_start(
+                        tab_s[32 * q : 32 * q + 4 * KP, :].bitcast(I32),
+                        tab_scales[:, 4 * q : 4 * q + 4, :].bitcast(I32),
+                    )
 
         def load_w1(b):
             if b == 0:
@@ -87,7 +87,7 @@ def tile_list_reassortment_watch_scores_kernel(
         w4_s = held.tile([P, HP, N], U8, name="w4_s", align_bytes=64)
         nc.vector.memset(w4_s[:].rearrange("p b n -> p (b n)").bitcast(I32), 0)
         for q in range(4):
-            nc.gpsimd.dma_start(
+            nc.sync.dma_start(
                 w4_s[32 * q : 32 * q + 4, :, :].bitcast(I32),
                 w4_scales[:, 4 * q : 4 * q + 4, :].rearrange("b r n -> r b n").bitcast(I32),
             )
@@ -102,6 +102,7 @@ def tile_list_reassortment_watch_scores_kernel(
         v_w.append(slots.tile([P, S], U32, name="v_w1", tag="tab_s", align_bytes=64))
         nc.vector.tensor_copy(v_w[1][:], tab_w[1][:].indirect(list1[:]))
 
+        last = HP - 1
         w1_q = {}
         banks_used = []
 
@@ -110,15 +111,19 @@ def tile_list_reassortment_watch_scores_kernel(
             banks_used.append(name)
             return bank
 
-        def prepare_first_w1(a, u):
+        woven_first = {}
+
+        def weave_first_w1(a, u):
             pairs = raw_w1[0][a].rearrange("p j (m u t) -> p u m j t", u=2, t=2)
-            woven = shared.tile(
-                [P, 2 * K_PASS], BF16, name="woven0%d%d" % (a, u), align_bytes=64, offset=4 * T + 4 * K_PASS * (2 * a + u)
-            )
-            nc.vector.tensor_copy(woven[:].rearrange("p (t m j) -> p m j t", t=2, j=PACK), pairs[:, u])
+            woven = two.tile([P, 2 * K_PASS], BF16, name="woven0", align_bytes=64)
+            copy = nc.vector.tensor_copy if (a, u) == (KP - 1, 0) else nc.scalar.copy
+            copy(woven[:].rearrange("p (t m j) -> p m j t", t=2, j=PACK), pairs[:, u])
+            woven_first[a, u] = woven
+
+        def quantize_first_w1(a, u):
             codes = held.tile([P, 2 * P], U32, name="w1_c0%d%d" % (a, u), align_bytes=64)
             scales = held.tile([P, 2 * P], U8, name="w1_s0%d%d" % (a, u), align_bytes=64)
-            nc.vector.quantize_mx(out=codes[:].bitcast(FP8X4), scales=scales[:], in_=woven[:])
+            nc.vector.quantize_mx(out=codes[:].bitcast(FP8X4), scales=scales[:], in_=woven_first[a, u][:])
             w1_q[0, a, u] = (codes[:], scales[:])
 
         def prepare_w1(b, u):
@@ -163,18 +168,19 @@ def tile_list_reassortment_watch_scores_kernel(
         xa = {}
         neg_xb = {}
 
-        def pick(b, i):
+        def pick(b, i, m0, m1):
             if i == 0:
-                xa_first[b] = two.tile([P, PACK - 1, M], F32, name="xa_first")
+                xa_first[b] = two.tile([P, PACK if b == last else PACK - 1, M], F32, name="xa_first")
                 neg_xb[b] = two.tile([P, PACK, M], F32, name="neg_xb")
-            if i < PACK - 1:
+            if i < PACK - 1 or b == last:
                 xa[b, i] = xa_first[b][:, i, :]
             else:
-                last = slots.tile([P, M], F32, name="xa_last", tag="h%d1" % (b % 2), align_bytes=64)
-                xa[b, i] = last[:]
+                held_back = slots.tile([P, M], F32, name="xa_last", tag="h%d1" % b, align_bytes=64)
+                xa[b, i] = held_back[:]
             h = h_tiles[b, i]
-            nc.vector.tensor_tensor(xa[b, i], h[:].indirect(list2[:]), wa[:], ALU.mult)
-            nc.vector.tensor_tensor(neg_xb[b][:, i, :], h[:].indirect(list3[:]), neg_wb[:], ALU.mult)
+            entries = slice(m0 // 16, m1 // 16)
+            nc.vector.tensor_tensor(xa[b, i][:, m0:m1], h[:].indirect(list2[:, entries]), wa[:, m0:m1], ALU.mult)
+            nc.vector.tensor_tensor(neg_xb[b][:, i, m0:m1], h[:].indirect(list3[:, entries]), neg_wb[:, m0:m1], ALU.mult)
 
         larger = {}
 
@@ -192,29 +198,39 @@ def tile_list_reassortment_watch_scores_kernel(
             nc.vector.scalar_tensor_tensor(
                 big[:, PACK - 1, :], neg_xb[b][:, PACK - 1, :], -1.0, xa[b, PACK - 1], ALU.mult, ALU.max
             )
-            larger[b] = big
+            for c in range(CHUNKS):
+                larger[b, c] = big[:, :, c * P : (c + 1) * P]
+
+        def take_larger_last(c):
+            big = two.tile([P, PACK, P], F32, name="big_last")
+            cols = slice(c * P, (c + 1) * P)
+            nc.vector.scalar_tensor_tensor(
+                big[:], neg_xb[last][:, :, cols], -1.0, xa_first[last][:, :, cols], ALU.mult, ALU.max
+            )
+            larger[last, c] = big[:]
 
         diffs = {}
 
-        def take_difference(b, i):
-            turned = next_bank([P, CHUNKS, P], "turned")
-            for c in range(CHUNKS):
+        def take_difference(b, i, c0, c1):
+            turned = next_bank([P, c1 - c0, P], "turned")
+            for c in range(c0, c1):
                 cols = slice(c * P, (c + 1) * P)
-                nc.tensor.matmul(turned[:, c, :], xa[b, i][:, cols], ident[:], is_transpose=True, start=True, stop=False)
-                nc.tensor.matmul(turned[:, c, :], neg_xb[b][:, i, cols], ident[:], is_transpose=True, start=False, stop=True)
-            staged = four.tile([P, CHUNKS, P], F32, name="staged")
+                into = turned[:, c - c0, :]
+                nc.tensor.matmul(into, xa[b, i][:, cols], ident[:], is_transpose=True, start=True, stop=False)
+                nc.tensor.matmul(into, neg_xb[b][:, i, cols], ident[:], is_transpose=True, start=False, stop=True)
+            staged = four.tile([P, c1 - c0, P], F32, name="staged")
             nc.scalar.copy(staged[:], turned[:])
-            for c in range(CHUNKS):
+            for c in range(c0, c1):
                 if i == 0:
                     diffs[b, c] = psum.tile([P, PACK, P], F32, name="diff", tag="diff%d" % c)
-                nc.tensor.transpose(diffs[b, c][:, i, :], staged[:, c, :], ident[:])
+                nc.tensor.transpose(diffs[b, c][:, i, :], staged[:, c - c0, :], ident[:])
 
         def multiply(b, c, z_cols):
             walk = "p i (c j) -> p c i j"
             nc.vector.tensor_tensor(
                 z_cols.rearrange("p (c j i) -> p c i j", j=2, i=PACK),
                 diffs[b, c][:].rearrange(walk, j=2),
-                larger[b][:, :, c * P : (c + 1) * P].rearrange(walk, j=2),
+                larger[b, c].rearrange(walk, j=2),
                 ALU.mult,
             )
 
@@ -260,38 +276,59 @@ def tile_list_reassortment_watch_scores_kernel(
 
         for a in range(KP):
             for u in range(2):
-                prepare_first_w1(a, u)
+                weave_first_w1(a, u)
+            for u in range(2):
+                quantize_first_w1(a, u)
         nc.vector.tensor_scalar(neg_wb[:], wb[:], -1.0, None, ALU.mult)
 
-        last = HP - 1
-        for b in range(HP):
+        for b in range(last):
             for i in range(PACK):
                 make_h(b, i)
                 if i < PACK - 1:
-                    pick(b, i)
-            if b < last:
-                prepare_w1(b + 1, 0)
-            pick(b, PACK - 1)
+                    pick(b, i, 0, M)
+            prepare_w1(b + 1, 0)
+            pick(b, PACK - 1, 0, M)
             take_larger(b)
             for i in range(PACK):
-                if b < last and i == 2:
+                if i == 2:
                     prepare_w1(b + 1, 1)
-                take_difference(b, i)
-            if b < last:
-                combine(b)
+                take_difference(b, i, 0, CHUNKS)
+            combine(b)
 
+        for i in range(PACK):
+            make_h(last, i)
+            if i < PACK - 1:
+                pick(last, i, 0, M)
+        pick(last, PACK - 1, 0, M // 2)
+        pick(last, PACK - 1, M // 2, M)
+        for i in range(PACK - 1):
+            take_difference(last, i, 0, CHUNKS)
+        take_difference(last, PACK - 1, 0, CHUNKS // 2)
+        take_difference(last, PACK - 1, CHUNKS // 2, CHUNKS)
         for c in range(CHUNKS):
             for b in range(last):
                 score_pass(b, c)
-        z_last = []
-        for c in range(CHUNKS):
-            z = four.tile([P, PACK * P], BF16, name="z_last", align_bytes=64)
-            multiply(last, c, z[:])
-            z_last.append(z)
-            if c > 0:
-                quantize_z(last, c - 1, z_last[c - 1])
-                score_pass(last, c - 1)
-                finish(c - 1)
-        quantize_z(last, CHUNKS - 1, z_last[CHUNKS - 1])
-        score_pass(last, CHUNKS - 1)
-        finish(CHUNKS - 1)
+
+        z_last = {}
+
+        def multiply_last(c):
+            z_last[c] = four.tile([P, PACK * P], BF16, name="z_last", align_bytes=64)
+            multiply(last, c, z_last[c][:])
+
+        def finish_last(c):
+            quantize_z(last, c, z_last[c])
+            score_pass(last, c)
+            finish(c)
+
+        take_larger_last(0)
+        take_larger_last(1)
+        multiply_last(0)
+        multiply_last(1)
+        finish_last(0)
+        take_larger_last(2)
+        finish_last(1)
+        multiply_last(2)
+        take_larger_last(3)
+        finish_last(2)
+        multiply_last(3)
+        finish_last(3)

@@ -24,6 +24,7 @@ BANK = 512
 KP = K // K_PASS
 HP = H // K_PASS
 CHUNKS = M // P
+FIRST_PART = T // 4
 GAIN_ON_VECTOR = 2
 
 
@@ -35,6 +36,7 @@ def tile_list_reassortment_watch_scores_kernel(
         held = ctx.enter_context(tc.tile_pool(name="held", bufs=1))
         two = ctx.enter_context(tc.tile_pool(name="two", bufs=2))
         four = ctx.enter_context(tc.tile_pool(name="four", bufs=4))
+        early = ctx.enter_context(tc.tile_pool(name="early", bufs=1))
         slots = ctx.enter_context(tc.tile_pool(name="slots", bufs=1))
         psum = ctx.enter_context(tc.psum_pool(name="psum", bufs=1))
 
@@ -43,29 +45,30 @@ def tile_list_reassortment_watch_scores_kernel(
         list3 = held.tile([P, M // 16], U16, name="list3")
         nc.sync.dma_start(list1[:], offs)
 
+        tab_s = early.tile([P, KP * T], U8, name="tab_s", align_bytes=64, offset=0)
+        nc.vector.memset(tab_s[:, :T].bitcast(I32), 0)
+        nc.gpsimd.memset(tab_s[:, T:].bitcast(I32), 0)
         ident = held.tile([P, P], F32, name="ident")
         make_identity(nc, ident[:])
 
-        tab_s = slots.tile([P, T], U8, name="tab_s", tag="tab_s", align_bytes=64)
-        nc.vector.memset(tab_s[:].bitcast(I32), 0)
-        tab_w = []
-        for a in range(KP):
-            words = held.tile([P, T], U32, name="tab_w%d" % a, align_bytes=64)
-            nc.sync.dma_start(words[:].bitcast(I32), tab_words[a].rearrange("p t i -> p (t i)").bitcast(I32))
-            tab_w.append(words)
-            if a == 0:
-                for q in range(4):
-                    nc.sync.dma_start(
-                        tab_s[32 * q : 32 * q + 4 * KP, :].bitcast(I32),
-                        tab_scales[:, 4 * q : 4 * q + 4, :].bitcast(I32),
-                    )
+        tab_w = [slots.tile([P, T], U32, name="tab_w", tag="wide%d" % a, align_bytes=64) for a in range(KP)]
+        tab_rows = [tab_words[a].rearrange("p t i -> p (t i)").bitcast(I32) for a in range(KP)]
+        nc.sync.dma_start(tab_w[0][:, :FIRST_PART].bitcast(I32), tab_rows[0][:, :FIRST_PART])
+        nc.sync.dma_start(
+            tab_s[0:P:8, :].bitcast(I32).rearrange("q (a t) -> q a t", a=KP),
+            tab_scales.rearrange("a q t -> q a t").bitcast(I32),
+        )
+        nc.sync.dma_start(list2[:], offs2)
+        nc.sync.dma_start(list3[:], offs3)
+        nc.sync.dma_start(tab_w[0][:, FIRST_PART:].bitcast(I32), tab_rows[0][:, FIRST_PART:])
+        nc.sync.dma_start(tab_w[1][:].bitcast(I32), tab_rows[1])
 
         def load_w1(b):
             if b == 0:
                 parts = [held.tile([P, PACK, K_PASS], F32, name="raw0%d" % a)[:] for a in range(KP)]
                 whole = None
             else:
-                whole = held.tile([P, KP, PACK, K_PASS], F32, name="raw%d" % b)
+                whole = slots.tile([P, KP, PACK, K_PASS], F32, name="raw", tag="wide%d" % (b - 1), align_bytes=64)
                 parts = [whole[:, a] for a in range(KP)]
             for a in range(KP):
                 rows = w1[a * K_PASS : (a + 1) * K_PASS, b * K_PASS : (b + 1) * K_PASS]
@@ -74,33 +77,36 @@ def tile_list_reassortment_watch_scores_kernel(
 
         raw_w1 = {0: load_w1(0)}
 
-        gain_sb = held.tile([P, HP, PACK], F32, name="gain_sb")
-        wa = held.tile([P, M], F32, name="wa")
-        wb = held.tile([P, M], F32, name="wb")
-        nc.sync.dma_start(list2[:], offs2)
+        picked_s = held.tile([P, KP * S], U8, name="picked_s", align_bytes=64)
+        for a in range(KP):
+            nc.vector.tensor_copy(picked_s[:, a * S : (a + 1) * S], tab_s[:, a * T : (a + 1) * T].indirect(list1[:]))
+        v_s = held.tile([P, KP * S], U8, name="v_s", align_bytes=64)
+        nc.gpsimd.memset(v_s[:].bitcast(I32), 0)
+        for q in range(4):
+            nc.sync.dma_start(v_s[32 * q : 32 * q + 4, :].bitcast(I32), picked_s[32 * q : 32 * q + 32 : 8, :].bitcast(I32))
+        v_w = []
+        for a in range(KP):
+            words = held.tile([P, S], U32, name="v_w%d" % a, align_bytes=64)
+            nc.vector.tensor_copy(words[:], tab_w[a][:].indirect(list1[:]))
+            v_w.append(words)
+
+        gain_sb = early.tile([P, HP, PACK], F32, name="gain_sb", align_bytes=64, offset=0)
+        wa = early.tile([P, M], F32, name="wa", align_bytes=64, offset=64)
+        wb = early.tile([P, M], F32, name="wb", align_bytes=64, offset=64 + 4 * M)
+        w4_s = early.tile([P, HP, N], U8, name="w4_s", align_bytes=64, offset=64 + 8 * M)
+        w4_w = early.tile([P, HP, 2 * N], U8, name="w4_w", align_bytes=64, offset=64 + 8 * M + HP * N)
         nc.sync.dma_start(gain_sb[:], gain.rearrange("(b p i) -> p b i", p=P, i=PACK))
         nc.sync.dma_start(wa[:], wga)
-        nc.sync.dma_start(list3[:], offs3)
         nc.sync.dma_start(wb[:], wgb)
         raw_w1[1] = load_w1(1)
-
-        w4_s = held.tile([P, HP, N], U8, name="w4_s", align_bytes=64)
-        nc.vector.memset(w4_s[:].rearrange("p b n -> p (b n)").bitcast(I32), 0)
+        nc.gpsimd.memset(w4_s[:].rearrange("p b n -> p (b n)").bitcast(I32), 0)
         for q in range(4):
             nc.sync.dma_start(
                 w4_s[32 * q : 32 * q + 4, :, :].bitcast(I32),
                 w4_scales[:, 4 * q : 4 * q + 4, :].rearrange("b r n -> r b n").bitcast(I32),
             )
-        w4_w = held.tile([P, HP, 2 * N], U8, name="w4_w", align_bytes=64)
-        nc.sync.dma_start(w4_w[:].bitcast(I32), w4_words.rearrange("b p c -> p b c").bitcast(I32))
         raw_w1[2] = load_w1(2)
-
-        v_w = [held.tile([P, S], U32, name="v_w0", align_bytes=64)]
-        v_s = held.tile([P, S], U8, name="v_s", align_bytes=64)
-        nc.vector.tensor_copy(v_w[0][:], tab_w[0][:].indirect(list1[:]))
-        nc.vector.tensor_copy(v_s[:], tab_s[:].indirect(list1[:]))
-        v_w.append(slots.tile([P, S], U32, name="v_w1", tag="tab_s", align_bytes=64))
-        nc.vector.tensor_copy(v_w[1][:], tab_w[1][:].indirect(list1[:]))
+        nc.sync.dma_start(w4_w[:].bitcast(I32), w4_words.rearrange("b p c -> p b c").bitcast(I32))
 
         last = HP - 1
         w1_q = {}
@@ -152,7 +158,7 @@ def tile_list_reassortment_watch_scores_kernel(
                         lhsT=codes[:, cols].bitcast(FP8X4),
                         lhsT_scale=scales[:, cols],
                         rhs=v_w[a][:, s0 : s0 + BANK].bitcast(FP8X4),
-                        rhs_scale=v_s[4 * a :, s0 : s0 + BANK],
+                        rhs_scale=v_s[:, a * S + s0 : a * S + s0 + BANK],
                         start=(a == 0),
                         stop=(a == KP - 1),
                     )
@@ -299,6 +305,8 @@ def tile_list_reassortment_watch_scores_kernel(
             make_h(last, i)
             if i < PACK - 1:
                 pick(last, i, 0, M)
+        warm = held.tile([P, 1], F32, name="warm")
+        nc.scalar.activation(warm[:], h_tiles[last, PACK - 1][:, 0:1], ACT.Sqrt, scale=0.0)
         pick(last, PACK - 1, 0, M // 2)
         pick(last, PACK - 1, M // 2, M)
         for i in range(PACK - 1):

from contextlib import ExitStack

import concourse.mybir as mybir
from concourse.masks import make_identity

K, T, S, H, M, N = 1024, 4096, 1024, 1536, 512, 384
FLOPS = 2 * K * H * S + 2 * H * N * M

F32 = mybir.dt.float32
BF16 = mybir.dt.bfloat16
I32 = mybir.dt.int32
U32 = mybir.dt.uint32
U16 = mybir.dt.uint16
U8 = mybir.dt.uint8
FP8X4 = mybir.dt.float8_e4m3fn_x4
FP4X4 = mybir.dt.float4_e2m1fn_x4
ALU = mybir.AluOpType
ACT = mybir.ActivationFunctionType

P = 128
PACK = 4
K_PASS = P * PACK
BANK = 512
KP = K // K_PASS
HP = H // K_PASS
CHUNKS = M // P
FIRST_PART = T // 4
GAIN_ON_VECTOR = 2


def tile_list_reassortment_watch_scores_kernel(
    tc, tab_words, tab_scales, offs, w1, gain, offs2, offs3, wga, wgb, w4_words, w4_scales, out
):
    nc = tc.nc
    with ExitStack() as ctx:
        held = ctx.enter_context(tc.tile_pool(name="held", bufs=1))
        two = ctx.enter_context(tc.tile_pool(name="two", bufs=2))
        four = ctx.enter_context(tc.tile_pool(name="four", bufs=4))
        early = ctx.enter_context(tc.tile_pool(name="early", bufs=1))
        slots = ctx.enter_context(tc.tile_pool(name="slots", bufs=1))
        psum = ctx.enter_context(tc.psum_pool(name="psum", bufs=1))

        list1 = held.tile([P, S // 16], U16, name="list1")
        list2 = held.tile([P, M // 16], U16, name="list2")
        list3 = held.tile([P, M // 16], U16, name="list3")
        nc.sync.dma_start(list1[:], offs)

        tab_s = early.tile([P, KP * T], U8, name="tab_s", align_bytes=64, offset=0)
        nc.vector.memset(tab_s[:, :T].bitcast(I32), 0)
        nc.gpsimd.memset(tab_s[:, T:].bitcast(I32), 0)
        ident = held.tile([P, P], F32, name="ident")
        make_identity(nc, ident[:])

        tab_w = [slots.tile([P, T], U32, name="tab_w", tag="wide%d" % a, align_bytes=64) for a in range(KP)]
        tab_rows = [tab_words[a].rearrange("p t i -> p (t i)").bitcast(I32) for a in range(KP)]
        nc.sync.dma_start(tab_w[0][:, :FIRST_PART].bitcast(I32), tab_rows[0][:, :FIRST_PART])
        nc.sync.dma_start(
            tab_s[0:P:8, :].bitcast(I32).rearrange("q (a t) -> q a t", a=KP),
            tab_scales.rearrange("a q t -> q a t").bitcast(I32),
        )
        nc.sync.dma_start(list2[:], offs2)
        nc.sync.dma_start(list3[:], offs3)
        nc.sync.dma_start(tab_w[0][:, FIRST_PART:].bitcast(I32), tab_rows[0][:, FIRST_PART:])
        nc.sync.dma_start(tab_w[1][:].bitcast(I32), tab_rows[1])

        def load_w1(b):
            if b == 0:
                parts = [held.tile([P, PACK, K_PASS], F32, name="raw0%d" % a)[:] for a in range(KP)]
                whole = None
            else:
                whole = slots.tile([P, KP, PACK, K_PASS], F32, name="raw", tag="wide%d" % (b - 1), align_bytes=64)
                parts = [whole[:, a] for a in range(KP)]
            for a in range(KP):
                rows = w1[a * K_PASS : (a + 1) * K_PASS, b * K_PASS : (b + 1) * K_PASS]
                nc.sync.dma_start(parts[a], rows.rearrange("(p j) c -> p j c", j=PACK))
            return parts if b == 0 else whole

        raw_w1 = {0: load_w1(0)}

        picked_s = held.tile([P, KP * S], U8, name="picked_s", align_bytes=64)
        for a in range(KP):
            nc.vector.tensor_copy(picked_s[:, a * S : (a + 1) * S], tab_s[:, a * T : (a + 1) * T].indirect(list1[:]))
        v_s = held.tile([P, KP * S], U8, name="v_s", align_bytes=64)
        nc.gpsimd.memset(v_s[:].bitcast(I32), 0)
        for q in range(4):
            nc.sync.dma_start(v_s[32 * q : 32 * q + 4, :].bitcast(I32), picked_s[32 * q : 32 * q + 32 : 8, :].bitcast(I32))
        v_w = []
        for a in range(KP):
            words = held.tile([P, S], U32, name="v_w%d" % a, align_bytes=64)
            nc.vector.tensor_copy(words[:], tab_w[a][:].indirect(list1[:]))
            v_w.append(words)

        gain_sb = early.tile([P, HP, PACK], F32, name="gain_sb", align_bytes=64, offset=0)
        wa = early.tile([P, M], F32, name="wa", align_bytes=64, offset=64)
        wb = early.tile([P, M], F32, name="wb", align_bytes=64, offset=64 + 4 * M)
        w4_s = early.tile([P, HP, N], U8, name="w4_s", align_bytes=64, offset=64 + 8 * M)
        w4_w = early.tile([P, HP, 2 * N], U8, name="w4_w", align_bytes=64, offset=64 + 8 * M + HP * N)
        nc.sync.dma_start(gain_sb[:], gain.rearrange("(b p i) -> p b i", p=P, i=PACK))
        nc.sync.dma_start(wa[:], wga)
        nc.sync.dma_start(wb[:], wgb)
        raw_w1[1] = load_w1(1)
        nc.gpsimd.memset(w4_s[:].rearrange("p b n -> p (b n)").bitcast(I32), 0)
        for q in range(4):
            nc.sync.dma_start(
                w4_s[32 * q : 32 * q + 4, :, :].bitcast(I32),
                w4_scales[:, 4 * q : 4 * q + 4, :].rearrange("b r n -> r b n").bitcast(I32),
            )
        raw_w1[2] = load_w1(2)
        nc.sync.dma_start(w4_w[:].bitcast(I32), w4_words.rearrange("b p c -> p b c").bitcast(I32))

        last = HP - 1
        w1_q = {}
        banks_used = []

        def next_bank(shape, name):
            bank = psum.tile(shape, F32, name=name, tag="work%d" % (len(banks_used) % 4))
            banks_used.append(name)
            return bank

        woven_first = {}

        def weave_first_w1(a, u):
            pairs = raw_w1[0][a].rearrange("p j (m u t) -> p u m j t", u=2, t=2)
            woven = two.tile([P, 2 * K_PASS], BF16, name="woven0", align_bytes=64)
            copy = nc.vector.tensor_copy if (a, u) == (KP - 1, 0) else nc.scalar.copy
            copy(woven[:].rearrange("p (t m j) -> p m j t", t=2, j=PACK), pairs[:, u])
            woven_first[a, u] = woven

        def quantize_first_w1(a, u):
            codes = held.tile([P, 2 * P], U32, name="w1_c0%d%d" % (a, u), align_bytes=64)
            scales = held.tile([P, 2 * P], U8, name="w1_s0%d%d" % (a, u), align_bytes=64)
            nc.vector.quantize_mx(out=codes[:].bitcast(FP8X4), scales=scales[:], in_=woven_first[a, u][:])
            w1_q[0, a, u] = (codes[:], scales[:])

        def prepare_w1(b, u):
            pairs = raw_w1[b][:].rearrange("p a j (m u t) -> p u a m j t", u=2, t=2)
            woven = slots.tile([P, KP * 2 * K_PASS], BF16, name="woven", tag="h%d%d" % (b - 1, u + 1), align_bytes=64)
            nc.scalar.copy(woven[:].rearrange("p (a t m j) -> p a m j t", a=KP, t=2, j=PACK), pairs[:, u])
            codes = held.tile([P, KP * 2 * P], U32, name="w1_c%d%d" % (b, u), align_bytes=64)
            scales = held.tile([P, KP * 2 * P], U8, name="w1_s%d%d" % (b, u), align_bytes=64)
            nc.vector.quantize_mx(out=codes[:].bitcast(FP8X4), scales=scales[:], in_=woven[:])
            for a in range(KP):
                w1_q[b, a, u] = (codes[:, a * 2 * P : (a + 1) * 2 * P], scales[:, a * 2 * P : (a + 1) * 2 * P])

        h_tiles = {}

        def make_h(b, i):
            h = slots.tile([P, S], F32, name="h", tag="h%d%d" % (b % 2, i), align_bytes=64)
            cols = slice((i % 2) * P, (i % 2 + 1) * P)
            factor = gain_sb[:, b, i : i + 1]
            on_vector = PACK * b + i < GAIN_ON_VECTOR
            for s0 in range(0, S, BANK):
                acc = next_bank([P, BANK], "acc")
                for a in range(KP):
                    codes, scales = w1_q[b, a, i // 2]
                    nc.tensor.matmul_mx(
                        out=acc[:],
                        lhsT=codes[:, cols].bitcast(FP8X4),
                        lhsT_scale=scales[:, cols],
                        rhs=v_w[a][:, s0 : s0 + BANK].bitcast(FP8X4),
                        rhs_scale=v_s[:, a * S + s0 : a * S + s0 + BANK],
                        start=(a == 0),
                        stop=(a == KP - 1),
                    )
                nc.scalar.activation(h[:, s0 : s0 + BANK], acc[:], ACT.Tanh)
                if on_vector:
                    nc.vector.tensor_scalar(h[:, s0 : s0 + BANK], h[:, s0 : s0 + BANK], factor, None, ALU.mult)
            if not on_vector:
                nc.scalar.activation(h[:], h[:], ACT.Copy, scale=factor)
            h_tiles[b, i] = h

        neg_wb = held.tile([P, M], F32, name="neg_wb")
        xa_first = {}
        xa = {}
        neg_xb = {}

        def pick(b, i, m0, m1):
            if i == 0:
                xa_first[b] = two.tile([P, PACK if b == last else PACK - 1, M], F32, name="xa_first")
                neg_xb[b] = two.tile([P, PACK, M], F32, name="neg_xb")
            if i < PACK - 1 or b == last:
                xa[b, i] = xa_first[b][:, i, :]
            else:
                held_back = slots.tile([P, M], F32, name="xa_last", tag="h%d1" % b, align_bytes=64)
                xa[b, i] = held_back[:]
            h = h_tiles[b, i]
            entries = slice(m0 // 16, m1 // 16)
            nc.vector.tensor_tensor(xa[b, i][:, m0:m1], h[:].indirect(list2[:, entries]), wa[:, m0:m1], ALU.mult)
            nc.vector.tensor_tensor(neg_xb[b][:, i, m0:m1], h[:].indirect(list3[:, entries]), neg_wb[:, m0:m1], ALU.mult)

        larger = {}

        def take_larger(b):
            big = slots.tile([P, PACK, M], F32, name="big", tag="h%d%d" % (b % 2, PACK - 1), align_bytes=64)
            flat = "p i m -> p (i m)"
            nc.vector.scalar_tensor_tensor(
                big[:, : PACK - 1, :].rearrange(flat),
                neg_xb[b][:, : PACK - 1, :].rearrange(flat),
                -1.0,
                xa_first[b][:].rearrange(flat),
                ALU.mult,
                ALU.max,
            )
            nc.vector.scalar_tensor_tensor(
                big[:, PACK - 1, :], neg_xb[b][:, PACK - 1, :], -1.0, xa[b, PACK - 1], ALU.mult, ALU.max
            )
            for c in range(CHUNKS):
                larger[b, c] = big[:, :, c * P : (c + 1) * P]

        def take_larger_last(c):
            big = two.tile([P, PACK, P], F32, name="big_last")
            cols = slice(c * P, (c + 1) * P)
            nc.vector.scalar_tensor_tensor(
                big[:], neg_xb[last][:, :, cols], -1.0, xa_first[last][:, :, cols], ALU.mult, ALU.max
            )
            larger[last, c] = big[:]

        diffs = {}

        def take_difference(b, i, c0, c1):
            turned = next_bank([P, c1 - c0, P], "turned")
            for c in range(c0, c1):
                cols = slice(c * P, (c + 1) * P)
                into = turned[:, c - c0, :]
                nc.tensor.matmul(into, xa[b, i][:, cols], ident[:], is_transpose=True, start=True, stop=False)
                nc.tensor.matmul(into, neg_xb[b][:, i, cols], ident[:], is_transpose=True, start=False, stop=True)
            staged = four.tile([P, c1 - c0, P], F32, name="staged")
            nc.scalar.copy(staged[:], turned[:])
            for c in range(c0, c1):
                if i == 0:
                    diffs[b, c] = psum.tile([P, PACK, P], F32, name="diff", tag="diff%d" % c)
                nc.tensor.transpose(diffs[b, c][:, i, :], staged[:, c - c0, :], ident[:])

        def multiply(b, c, z_cols):
            walk = "p i (c j) -> p c i j"
            nc.vector.tensor_tensor(
                z_cols.rearrange("p (c j i) -> p c i j", j=2, i=PACK),
                diffs[b, c][:].rearrange(walk, j=2),
                larger[b, c].rearrange(walk, j=2),
                ALU.mult,
            )

        z_q = {}

        def quantize_z(b, c0, z):
            width = z.shape[1] // PACK
            codes = held.tile([P, width], U32, name="z_c%d%d" % (b, c0), align_bytes=64)
            scales = held.tile([P, width], U8, name="z_s%d%d" % (b, c0), align_bytes=64)
            nc.vector.quantize_mx(out=codes[:].bitcast(FP8X4), scales=scales[:], in_=z[:])
            for c in range(width // P):
                z_q[b, c0 + c] = (codes[:, c * P : (c + 1) * P], scales[:, c * P : (c + 1) * P])

        def combine(b):
            z = held.tile([P, PACK * M], BF16, name="z", align_bytes=64)
            for c in range(CHUNKS):
                multiply(b, c, z[:, c * PACK * P : (c + 1) * PACK * P])
            quantize_z(b, 0, z)

        y_banks = {}

        def score_pass(b, c):
            codes, scales = z_q[b, c]
            if b == 0:
                y_banks[c] = next_bank([P, N // P, P], "y")
            for n in range(N // P):
                nc.tensor.matmul_mx(
                    out=y_banks[c][:, n, :],
                    lhsT=w4_w[:, b, 2 * P * n : 2 * P * (n + 1)].bitcast(FP4X4),
                    lhsT_scale=w4_s[:, b, P * n : P * (n + 1)],
                    rhs=codes.bitcast(FP8X4),
                    rhs_scale=scales,
                    start=(b == 0 and n == 0),
                    stop=(b == HP - 1 and n == N // P - 1),
                )

        def finish(c):
            size = two.tile([P, N // P, P], F32, name="size")
            nc.scalar.activation(size[:], y_banks[c][:], ACT.Abs)
            root = four.tile([P, N // P, P], F32, name="root")
            nc.scalar.activation(root[:], size[:], ACT.Sqrt)
            nc.sync.dma_start(out[:, c * P : (c + 1) * P].rearrange("(n p) m -> p n m", p=P), root[:])

        for a in range(KP):
            for u in range(2):
                weave_first_w1(a, u)
            for u in range(2):
                quantize_first_w1(a, u)
        nc.vector.tensor_scalar(neg_wb[:], wb[:], -1.0, None, ALU.mult)

        for b in range(last):
            for i in range(PACK):
                make_h(b, i)
                if i < PACK - 1:
                    pick(b, i, 0, M)
            prepare_w1(b + 1, 0)
            pick(b, PACK - 1, 0, M)
            take_larger(b)
            for i in range(PACK):
                if i == 2:
                    prepare_w1(b + 1, 1)
                take_difference(b, i, 0, CHUNKS)
            combine(b)

        for i in range(PACK):
            make_h(last, i)
            if i < PACK - 1:
                pick(last, i, 0, M)
        warm = held.tile([P, 1], F32, name="warm")
        nc.scalar.activation(warm[:], h_tiles[last, PACK - 1][:, 0:1], ACT.Sqrt, scale=0.0)
        pick(last, PACK - 1, 0, M // 2)
        pick(last, PACK - 1, M // 2, M)
        for i in range(PACK - 1):
            take_difference(last, i, 0, CHUNKS)
        take_difference(last, PACK - 1, 0, CHUNKS // 2)
        take_difference(last, PACK - 1, CHUNKS // 2, CHUNKS)
        for c in range(CHUNKS):
            for b in range(last):
                score_pass(b, c)

        z_last = {}

        def multiply_last(c):
            z_last[c] = four.tile([P, PACK * P], BF16, name="z_last", align_bytes=64)
            multiply(last, c, z_last[c][:])

        def finish_last(c):
            quantize_z(last, c, z_last[c])
            score_pass(last, c)
            finish(c)

        take_larger_last(0)
        take_larger_last(1)
        multiply_last(0)
        multiply_last(1)
        finish_last(0)
        take_larger_last(2)
        finish_last(1)
        multiply_last(2)
        take_larger_last(3)
        finish_last(2)
        multiply_last(3)
        finish_last(3)
